import numpy as np
import ml_dtypes


def mxq(x, axis, fmt="e4m3"):
    dtype, down = {"e4m3": (ml_dtypes.float8_e4m3fn, 7), "e5m2": (ml_dtypes.float8_e5m2, 14)}[fmt]
    v = np.moveaxis(np.asarray(x, np.float32).astype(ml_dtypes.bfloat16).astype(np.float64), axis, -1)
    blocks = v.reshape(v.shape[:-1] + (-1, 32))
    amax = np.abs(blocks).max(-1, keepdims=True)
    byte = np.maximum(np.where(amax > 0, np.frexp(amax)[1] - 1 + 127, 0) - down, 1)
    scale = np.exp2(byte - 127.0)
    codes = (blocks / scale).astype(np.float32).astype(dtype).astype(np.float64)
    return np.moveaxis((codes * scale).reshape(v.shape), -1, axis)


WIDE = False


def mx_kscale(k):
    if not WIDE:
        return np.ones(k)
    levels = np.array([10, -10, 5, -5, 0])
    if k % 512:
        return np.exp2(np.random.permutation(np.resize(levels, k // 32))).repeat(32)
    a = np.empty((k // 512, 16))
    for p in range(k // 512):
        a[p, :8] = np.random.permutation(np.resize(levels, 8))
        for g in range(8):
            far = levels[np.abs(levels - a[p, g]) >= 10]
            a[p, g + 8] = far[np.random.randint(len(far))]
    return np.exp2(a.ravel()).repeat(32)


def f64(x):
    return np.asarray(x).astype(np.float64)


def striped(idx):
    return np.tile(idx.reshape(-1, 16).T, (8, 1)).astype(np.uint16)


def unstriped(offs):
    return offs[:16].T.reshape(-1).astype(np.int64)


def striped8(idx):
    return np.concatenate([x.reshape(-1, 16).T for x in idx]).astype(np.uint16)


def runs(offs, k):
    lists = np.stack([offs[16 * r : 16 * r + 16].T.reshape(-1) for r in range(8)]).astype(np.int64)
    return lists[np.arange(k) % 512 // 64]


def pack_weight(w):
    k, n = w.shape
    w = f64(np.asarray(w, np.float32).astype(ml_dtypes.bfloat16)).reshape(k // 32, 32, n)
    amax = np.abs(w).max(1)
    byte = np.clip(np.where(amax > 0, np.frexp(amax)[1] - 1 + 127 - 7, 1), 1, 254)
    scaled = (w * np.exp2(127.0 - byte)[:, None, :]).reshape(k, n).astype(np.float32)
    words = np.ascontiguousarray(scaled.reshape(k // 512, 128, 4, n).transpose(0, 1, 3, 2)).astype(ml_dtypes.float8_e4m3fn).view(np.uint8)
    return words, np.ascontiguousarray(byte.astype(np.uint8).reshape(k // 512, 16, n))


def unpack_weight(words, scales):
    g, p, n, _ = words.shape
    vals = np.ascontiguousarray(words).view(ml_dtypes.float8_e4m3fn).astype(np.float64) * np.repeat(np.exp2(scales.astype(np.float64) - 127.0), 8, axis=1)[..., None]
    return vals.transpose(0, 1, 3, 2).reshape(g * 512, n)

def planes(y):
    n, m = y.shape
    v = y.astype(np.float32).astype(ml_dtypes.bfloat16).astype(np.float64).reshape(n // 32, 32, m)
    top = np.abs(v).max(1)
    byte = np.clip(np.where(top > 0, np.frexp(top)[1] - 1 + 127 - 7, 1), 1, 254)
    codes = (v * np.exp2(127.0 - byte)[:, None, :]).reshape(n, m).astype(np.float32).astype(ml_dtypes.float8_e4m3fn).view(np.uint8)
    words = codes.reshape(n // 512, 128, 4, m).transpose(0, 1, 3, 2)
    return np.ascontiguousarray(words), np.ascontiguousarray(byte.astype(np.uint8).reshape(n // 512, 16, m))


K, T, S, N, H, J = 512, 2048, 512, 512, 512, 512


def setup_inputs():
    n = np.random.standard_normal
    s = mx_kscale(K)[:, None]
    u = mx_kscale(H)
    packed_xT = pack_weight(n((K, T)) * s)
    packed_w1 = pack_weight(n((K, H)) / np.sqrt(K) / s)
    packed_w2 = pack_weight(n((H, N)) / np.sqrt(H) / u[:, None])
    return {
        "x_words": packed_xT[0],
        "x_scales": packed_xT[1],
        "w1_words": packed_w1[0],
        "w1_scales": packed_w1[1],
        "gn": (np.random.uniform(0.5, 1.5, (H, 1)) * u[:, None]).astype(np.float32),
        "w2_words": packed_w2[0],
        "w2_scales": packed_w2[1],
        "tab": n((N, J)).astype(np.float32),
        "offs": striped(np.random.permutation(T)[:S]),
        "n1": striped8(np.stack([np.random.permutation(S) for _ in range(8)])),
        "n2": striped8(np.stack([np.random.permutation(S) for _ in range(8)])),
        "n3": striped8(np.random.randint(0, J, (8, S))),
        "n4": striped8(np.random.randint(0, J, (8, S))),
        "n5": striped8(np.stack([np.random.permutation(S) for _ in range(8)])),
    }


def reference(x_words, x_scales, w1_words, w1_scales, gn, w2_words, w2_scales, tab, offs, n1, n2, n3, n4, n5):
    xq = unpack_weight(x_words, x_scales)[:, unstriped(offs)]
    y = unpack_weight(w1_words, w1_scales).T @ xq
    z = f64(gn) * ((np.tanh(y[np.arange(H)[:, None], runs(n1, H)] - y)) * (y[np.arange(H)[:, None], runs(n2, H)]))
    h = unpack_weight(w2_words, w2_scales).T @ mxq(z, 0, "e4m3")
    out_0 = (h[np.arange(N)[:, None], runs(n5, N)]) * (f64(tab)[np.arange(N)[:, None], runs(n3, N)]) + f64(tab)[np.arange(N)[:, None], runs(n4, N)]
    return (out_0,) + planes(out_0)

@@ -1,0 +1,212 @@
+from contextlib import ExitStack
+
+import concourse.mybir as mybir
+
+F32 = mybir.dt.float32
+BF16 = mybir.dt.bfloat16
+I32 = mybir.dt.int32
+U32 = mybir.dt.uint32
+U16 = mybir.dt.uint16
+U8 = mybir.dt.uint8
+FP8X4 = mybir.dt.float8_e4m3fn_x4
+ALU = mybir.AluOpType
+ACT = mybir.ActivationFunctionType
+
+P = 128
+PACK = 4
+T = 2048
+S = 512
+HALF = S // 2
+FLOPS = 2 * 2 * 512 * 512 * 512
+
+HALVES = [slice(0, 256), slice(256, 512)]
+OUT_CHUNKS = [slice(0, 256), slice(256, 384), slice(384, 512)]
+
+
+def entries(lst, cols):
+    return lst[:, cols.start // 16 : cols.stop // 16]
+
+
+def tile_picked_layfdifkinda_none_po_kernel(
+    tc, x_words, x_scales, w1_words, w1_scales, gn, w2_words, w2_scales, tab, offs, n1, n2, n3, n4, n5, out_0, out_1, out_2
+):
+    nc = tc.nc
+    with ExitStack() as ctx:
+        keep = ctx.enter_context(tc.tile_pool(name="keep", bufs=1))
+        psum = ctx.enter_context(tc.psum_pool(name="psum", bufs=1))
+
+        def sb(name, shape, dtype, tag=None):
+            return keep.tile(shape, dtype, name=name, tag=tag or name, align_bytes=64)
+
+        def bank(name, number, width):
+            return psum.tile([P, width], F32, name=name, tag="bank%d" % number)
+
+        def load_list(name, src):
+            lst = sb(name, [P, S // 16], U16)
+            nc.sync.dma_start(lst[:], src)
+            return lst
+
+        def load_words(name, src, width, tag):
+            words = sb(name, [P, width], I32, tag)
+            nc.sync.dma_start(words[:], src[0].rearrange("p n t -> p (n t)").bitcast(I32))
+            return words
+
+        def load_scales(queue, plane, src):
+            for q in range(4):
+                queue.dma_start(plane[32 * q : 32 * q + 4, :].bitcast(I32), src[0, 4 * q : 4 * q + 4, :].bitcast(I32))
+
+        tab_rows = tab.rearrange("(p t) j -> p t j", t=PACK)
+
+        def load_tab(t, tag):
+            rows = sb("tab%d" % t, [P, S], F32, tag)
+            nc.sync.dma_start(rows[:], tab_rows[:, t, :])
+            return rows
+
+        def deal(name, raw, dtype):
+            dealt = sb(name, [P, S], dtype)
+            nc.vector.tensor_copy(
+                dealt[:].rearrange("p (t m) -> p t m", t=PACK), raw[:].rearrange("p (m t) -> p t m", t=PACK)
+            )
+            return dealt
+
+        def product(acc, w_words, w_scales, t, a_words, a_scales, cols):
+            rows = slice(P * t, P * (t + 1))
+            nc.tensor.matmul_mx(
+                out=acc[:],
+                lhsT=w_words[:, rows].bitcast(FP8X4),
+                lhsT_scale=w_scales[:, rows],
+                rhs=a_words[:, cols].bitcast(FP8X4),
+                rhs_scale=a_scales[:, cols],
+                start=True,
+                stop=True,
+            )
+
+        def interleave(engine_copy, grouped, planes):
+            engine_copy(
+                grouped[:].rearrange("p (c i t) -> p c t i", i=4, t=PACK),
+                planes[:].rearrange("p t (c i) -> p c t i", i=4),
+            )
+
+        x_plane = sb("x_plane", [P, T], U8)
+        w_plane = sb("w_plane", [P, S], U8)
+        zero = sb("zero", [P, 1], F32)
+        no_bias = sb("no_bias", [P, 1], F32)
+        nc.gpsimd.memset(w_plane[:].bitcast(I32), 0)
+        nc.gpsimd.memset(x_plane[:].bitcast(I32), 0)
+        nc.vector.memset(zero[:], 0.0)
+        nc.scalar.activation(no_bias[:], zero[:], ACT.Tanh)
+
+        tabs = [None] * PACK
+        l3 = load_list("l3", n3)
+        tabs[0] = load_tab(0, None)
+        w1_raw = load_words("w1_raw", w1_words, S, "w_raw")
+        load_scales(nc.sync, w_plane, w1_scales)
+        x_raw = load_words("x_raw", x_words, T, None)
+        l0 = load_list("l0", offs)
+        load_scales(nc.sync, x_plane, x_scales)
+        l1 = load_list("l1", n1)
+        tabs[1] = load_tab(1, None)
+        l2 = load_list("l2", n2)
+        gain = sb("gain", [P, PACK], F32)
+        nc.sync.dma_start(gain[:], gn.rearrange("(p t) o -> p (t o)", t=PACK))
+        l5 = load_list("l5", n5)
+        l4 = load_list("l4", n4)
+
+        factors = [None] * PACK
+
+        def fetch_factor(t, tag):
+            factors[t] = sb("factor%d" % t, [P, S], F32, tag)
+            for cols in HALVES:
+                nc.vector.tensor_copy(factors[t][:, cols], tabs[t][:].indirect(entries(l3, cols)))
+
+        fetch_factor(0, None)
+        w1_codes = deal("w1_codes", w1_raw, I32)
+        w1_bytes = deal("w1_bytes", w_plane, U8)
+        w2_raw = load_words("w2_raw", w2_words, S, "w_raw")
+        load_scales(nc.sync, w_plane, w2_scales)
+
+        x_codes = sb("x_codes", [P, S], I32)
+        x_bytes = sb("x_bytes", [P, S], U8)
+        y_window = [sb("y_window%d" % t, [P, S], F32) for t in range(PACK)]
+        y_plain = [sb("y_plain%d" % t, [P, S], F32) for t in range(PACK)]
+        y_gained = [sb("y_gained%d" % t, [P, S], F32) for t in range(PACK)]
+        diff = [sb("diff%d" % t, [P, S], F32) for t in range(PACK)]
+        squash = [sb("squash%d" % t, [P, S], F32) for t in range(PACK)]
+
+        y_parts = []
+        for h, cols in enumerate(HALVES):
+            nc.vector.tensor_copy(x_codes[:, cols].bitcast(U32), x_raw[:].bitcast(U32).indirect(entries(l0, cols)))
+            nc.vector.tensor_copy(x_bytes[:, cols], x_plane[:].indirect(entries(l0, cols)))
+            acc = bank("y0_%d" % h, h, HALF)
+            product(acc, w1_codes, w1_bytes, 0, x_codes, x_bytes, cols)
+            y_parts.append((0, cols, acc))
+        for t in range(1, PACK):
+            acc = bank("y%d" % t, t + 1, S)
+            product(acc, w1_codes, w1_bytes, t, x_codes, x_bytes, slice(0, S))
+            y_parts.append((t, slice(0, S), acc))
+
+        tabs[2] = load_tab(2, "x_raw")
+        tabs[3] = load_tab(3, "x_plane")
+        fetch_factor(1, None)
+        w2_codes = deal("w2_codes", w2_raw, I32)
+        w2_bytes = deal("w2_bytes", w_plane, U8)
+
+        for t, cols, acc in y_parts:
+            nc.scalar.copy(y_window[t][:, cols], acc[:])
+            nc.scalar.copy(y_plain[t][:, cols], acc[:])
+        for t in range(PACK):
+            for cols in HALVES:
+                nc.vector.tensor_tensor(
+                    diff[t][:, cols], y_window[t][:].indirect(entries(l1, cols)), y_plain[t][:, cols], ALU.subtract
+                )
+
+        z_planes = [sb("z_planes%d" % h, [P, PACK, HALF], F32) for h in range(2)]
+        for h, cols in enumerate(HALVES):
+            for t in range(PACK):
+                if h == 0:
+                    for tt, part, acc in y_parts:
+                        if tt == t:
+                            nc.scalar.activation(y_gained[t][:, part], acc[:], ACT.Copy, scale=gain[:, t : t + 1])
+                nc.scalar.activation(squash[t][:, cols], diff[t][:, cols], ACT.Tanh, bias=no_bias[:])
+                nc.vector.tensor_tensor(
+                    z_planes[h][:, t, :], y_gained[t][:].indirect(entries(l2, cols)), squash[t][:, cols], ALU.mult
+                )
+
+        z_codes = sb("z_codes", [P, S], I32)
+        z_bytes = sb("z_bytes", [P, S], U8)
+        h_window = [sb("h_window%d" % t, [P, S], F32) for t in range(PACK)]
+        for h, cols in enumerate(HALVES):
+            grouped = sb("z_grouped%d" % h, [P, HALF * PACK], BF16)
+            interleave(nc.scalar.copy, grouped, z_planes[h])
+            nc.vector.quantize_mx(out=z_codes[:, cols].bitcast(FP8X4), scales=z_bytes[:, cols], in_=grouped[:])
+            for t in range(PACK):
+                acc = bank("h%d_%d" % (t, h), (5 + 4 * h + t) % 8, HALF)
+                product(acc, w2_codes, w2_bytes, t, z_codes, z_bytes, cols)
+                nc.scalar.copy(h_window[t][:, cols], acc[:])
+        fetch_factor(2, "squash2")
+        fetch_factor(3, "z_grouped1")
+
+        out_rows = out_0.rearrange("(p t) j -> p t j", t=PACK)
+        out_words = out_1[0].rearrange("p n t -> p (n t)").bitcast(I32)
+        o_codes = sb("o_codes", [P, S], I32)
+        o_bytes = sb("o_bytes", [P, S], U8)
+        scaled = [sb("scaled%d" % t, [P, S], F32) for t in range(PACK)]
+        for c, cols in enumerate(OUT_CHUNKS):
+            width = cols.stop - cols.start
+            planes = sb("o_planes%d" % c, [P, PACK, width], F32)
+            for t in range(PACK):
+                nc.vector.tensor_tensor(
+                    scaled[t][:, cols], h_window[t][:].indirect(entries(l5, cols)), factors[t][:, cols], ALU.mult
+                )
+            for t in range(PACK):
+                nc.vector.tensor_tensor(
+                    planes[:, t, :], tabs[t][:].indirect(entries(l4, cols)), scaled[t][:, cols], ALU.add
+                )
+            nc.sync.dma_start(out_rows[:, :, cols], planes[:])
+            grouped = sb("o_grouped%d" % c, [P, width * PACK], BF16)
+            interleave(nc.scalar.copy, grouped, planes)
+            nc.vector.quantize_mx(out=o_codes[:, cols].bitcast(FP8X4), scales=o_bytes[:, cols], in_=grouped[:])
+            nc.sync.dma_start(out_words[:, cols], o_codes[:, cols])
+        for q in range(4):
+            queue = nc.sync if q % 2 else nc.scalar
+            queue.dma_start(out_2[0, 4 * q : 4 * q + 4, :].bitcast(I32), o_bytes[32 * q : 32 * q + 4, :].bitcast(I32))

@@ -51,8 +51,8 @@ def tile_picked_layfdifkinda_none_po_kernel(
             nc.sync.dma_start(words[:], src[0].rearrange("p n t -> p (n t)").bitcast(I32))
             return words
 
-        def load_scales(queue, plane, src):
-            for q in range(4):
+        def load_scales(queue, plane, src, quadrants=range(4)):
+            for q in quadrants:
                 queue.dma_start(plane[32 * q : 32 * q + 4, :].bitcast(I32), src[0, 4 * q : 4 * q + 4, :].bitcast(I32))
 
         tab_rows = tab.rearrange("(p t) j -> p t j", t=PACK)
@@ -62,10 +62,11 @@ def tile_picked_layfdifkinda_none_po_kernel(
             nc.sync.dma_start(rows[:], tab_rows[:, t, :])
             return rows
 
-        def deal(name, raw, dtype):
-            dealt = sb(name, [P, S], dtype)
-            nc.vector.tensor_copy(
-                dealt[:].rearrange("p (t m) -> p t m", t=PACK), raw[:].rearrange("p (m t) -> p t m", t=PACK)
+        def deal(name, raw, dtype, run, tag=None):
+            dealt = sb(name, [P, S], dtype, tag)
+            nc.gpsimd.tensor_copy(
+                dealt[:].rearrange("p (t c i) -> p c t i", t=PACK, i=run),
+                raw[:].rearrange("p (c i t) -> p c t i", t=PACK, i=run),
             )
             return dealt
 
@@ -89,28 +90,33 @@ def tile_picked_layfdifkinda_none_po_kernel(
 
         x_plane = sb("x_plane", [P, T], U8)
         w_plane = sb("w_plane", [P, S], U8)
+        w2_plane = sb("w2_plane", [P, S], U8)
         zero = sb("zero", [P, 1], F32)
         no_bias = sb("no_bias", [P, 1], F32)
         nc.gpsimd.memset(w_plane[:].bitcast(I32), 0)
         nc.gpsimd.memset(x_plane[:].bitcast(I32), 0)
+        nc.gpsimd.memset(w2_plane[:].bitcast(I32), 0)
         nc.vector.memset(zero[:], 0.0)
         nc.scalar.activation(no_bias[:], zero[:], ACT.Tanh)
 
         tabs = [None] * PACK
         l3 = load_list("l3", n3)
         tabs[0] = load_tab(0, None)
-        w1_raw = load_words("w1_raw", w1_words, S, "w_raw")
-        load_scales(nc.sync, w_plane, w1_scales)
-        x_raw = load_words("x_raw", x_words, T, None)
+        l4 = load_list("l4", n4)
         l0 = load_list("l0", offs)
+        load_scales(nc.sync, w_plane, w1_scales, range(3))
+        x_raw = load_words("x_raw", x_words, T, None)
+        load_scales(nc.sync, w_plane, w1_scales, range(3, 4))
         load_scales(nc.sync, x_plane, x_scales)
-        l1 = load_list("l1", n1)
+        w1_raw = load_words("w1_raw", w1_words, S, None)
         tabs[1] = load_tab(1, None)
+        w2_raw = load_words("w2_raw", w2_words, S, None)
+        load_scales(nc.sync, w2_plane, w2_scales)
+        l1 = load_list("l1", n1)
         l2 = load_list("l2", n2)
         gain = sb("gain", [P, PACK], F32)
         nc.sync.dma_start(gain[:], gn.rearrange("(p t) o -> p (t o)", t=PACK))
         l5 = load_list("l5", n5)
-        l4 = load_list("l4", n4)
 
         factors = [None] * PACK
 
@@ -120,10 +126,13 @@ def tile_picked_layfdifkinda_none_po_kernel(
                 nc.vector.tensor_copy(factors[t][:, cols], tabs[t][:].indirect(entries(l3, cols)))
 
         fetch_factor(0, None)
-        w1_codes = deal("w1_codes", w1_raw, I32)
-        w1_bytes = deal("w1_bytes", w_plane, U8)
-        w2_raw = load_words("w2_raw", w2_words, S, "w_raw")
-        load_scales(nc.sync, w_plane, w2_scales)
+        term0 = sb("term0", [P, S], F32)
+        for cols in HALVES:
+            nc.vector.tensor_copy(term0[:, cols], tabs[0][:].indirect(entries(l4, cols)))
+        w1_bytes = deal("w1_bytes", w_plane, U8, 16)
+        w1_codes = deal("w1_codes", w1_raw, I32, 4)
+        w2_codes = deal("w2_codes", w2_raw, I32, 4)
+        w2_bytes = deal("w2_bytes", w2_plane, U8, 16)
 
         x_codes = sb("x_codes", [P, S], I32)
         x_bytes = sb("x_bytes", [P, S], U8)
@@ -148,8 +157,6 @@ def tile_picked_layfdifkinda_none_po_kernel(
         tabs[2] = load_tab(2, "x_raw")
         tabs[3] = load_tab(3, "x_plane")
         fetch_factor(1, None)
-        w2_codes = deal("w2_codes", w2_raw, I32)
-        w2_bytes = deal("w2_bytes", w_plane, U8)
 
         for t, cols, acc in y_parts:
             nc.scalar.copy(y_window[t][:, cols], acc[:])
@@ -198,13 +205,19 @@ def tile_picked_layfdifkinda_none_po_kernel(
                 nc.vector.tensor_tensor(
                     scaled[t][:, cols], h_window[t][:].indirect(entries(l5, cols)), factors[t][:, cols], ALU.mult
                 )
-            for t in range(PACK):
+            nc.vector.tensor_tensor(planes[:, 0, :], term0[:, cols], scaled[0][:, cols], ALU.add)
+            for t in range(1, PACK):
                 nc.vector.tensor_tensor(
                     planes[:, t, :], tabs[t][:].indirect(entries(l4, cols)), scaled[t][:, cols], ALU.add
                 )
             nc.sync.dma_start(out_rows[:, :, cols], planes[:])
             grouped = sb("o_grouped%d" % c, [P, width * PACK], BF16)
-            interleave(nc.scalar.copy, grouped, planes)
+            if c + 1 < len(OUT_CHUNKS):
+                interleave(nc.scalar.copy, grouped, planes)
+            else:
+                pairs = grouped[:].rearrange("p (n u e) -> p u n e", u=2, e=2)
+                nc.scalar.copy(pairs[:, 0], planes[:, 0:2, :].rearrange("p e n -> p n e"))
+                nc.vector.tensor_copy(pairs[:, 1], planes[:, 2:4, :].rearrange("p e n -> p n e"))
             nc.vector.quantize_mx(out=o_codes[:, cols].bitcast(FP8X4), scales=o_bytes[:, cols], in_=grouped[:])
             nc.sync.dma_start(out_words[:, cols], o_codes[:, cols])
         for q in range(4):

@@ -53,7 +53,7 @@ def tile_picked_layfdifkinda_none_po_kernel(
 
         def load_scales(queue, plane, src, quadrants=range(4)):
             for q in quadrants:
-                queue.dma_start(plane[32 * q : 32 * q + 4, :].bitcast(I32), src[0, 4 * q : 4 * q + 4, :].bitcast(I32))
+                queue.dma_start(plane[q:P:32, :].bitcast(I32), src[0, q:16:4, :].bitcast(I32))
 
         tab_rows = tab.rearrange("(p t) j -> p t j", t=PACK)
 
@@ -100,8 +100,8 @@ def tile_picked_layfdifkinda_none_po_kernel(
         nc.scalar.activation(no_bias[:], zero[:], ACT.Tanh)
 
         tabs = [None] * PACK
-        l3 = load_list("l3", n3)
         tabs[0] = load_tab(0, None)
+        l3 = load_list("l3", n3)
         l4 = load_list("l4", n4)
         l0 = load_list("l0", offs)
         load_scales(nc.sync, w_plane, w1_scales, range(3))
@@ -115,17 +115,17 @@ def tile_picked_layfdifkinda_none_po_kernel(
         l1 = load_list("l1", n1)
         l2 = load_list("l2", n2)
         gain = sb("gain", [P, PACK], F32)
-        nc.sync.dma_start(gain[:], gn.rearrange("(p t) o -> p (t o)", t=PACK))
+        nc.gpsimd.dma_start(gain[:], gn.rearrange("(p t) o -> p (t o)", t=PACK))
         l5 = load_list("l5", n5)
 
-        factors = [None] * PACK
+        factors = {}
 
-        def fetch_factor(t, tag):
+        def fetch_factor(t, tag=None):
             factors[t] = sb("factor%d" % t, [P, S], F32, tag)
             for cols in HALVES:
                 nc.vector.tensor_copy(factors[t][:, cols], tabs[t][:].indirect(entries(l3, cols)))
 
-        fetch_factor(0, None)
+        fetch_factor(0)
         term0 = sb("term0", [P, S], F32)
         for cols in HALVES:
             nc.vector.tensor_copy(term0[:, cols], tabs[0][:].indirect(entries(l4, cols)))
@@ -143,8 +143,8 @@ def tile_picked_layfdifkinda_none_po_kernel(
         squash = [sb("squash%d" % t, [P, S], F32) for t in range(PACK)]
 
         y_parts = []
+        nc.vector.tensor_copy(x_codes[:].bitcast(U32), x_raw[:].bitcast(U32).indirect(l0[:]))
         for h, cols in enumerate(HALVES):
-            nc.vector.tensor_copy(x_codes[:, cols].bitcast(U32), x_raw[:].bitcast(U32).indirect(entries(l0, cols)))
             nc.vector.tensor_copy(x_bytes[:, cols], x_plane[:].indirect(entries(l0, cols)))
             acc = bank("y0_%d" % h, h, HALF)
             product(acc, w1_codes, w1_bytes, 0, x_codes, x_bytes, cols)
@@ -156,28 +156,43 @@ def tile_picked_layfdifkinda_none_po_kernel(
 
         tabs[2] = load_tab(2, "x_raw")
         tabs[3] = load_tab(3, "x_plane")
-        fetch_factor(1, None)
+        fetch_factor(1)
 
-        for t, cols, acc in y_parts:
-            nc.scalar.copy(y_window[t][:, cols], acc[:])
-            nc.scalar.copy(y_plain[t][:, cols], acc[:])
-        for t in range(PACK):
+        z_planes = [sb("z_planes%d" % h, [P, PACK, HALF], F32) for h in range(2)]
+
+        def difference(t):
+            for tt, cols, acc in y_parts:
+                if tt == t:
+                    nc.scalar.copy(y_window[t][:, cols], acc[:])
+                    nc.scalar.copy(y_plain[t][:, cols], acc[:])
             for cols in HALVES:
                 nc.vector.tensor_tensor(
                     diff[t][:, cols], y_window[t][:].indirect(entries(l1, cols)), y_plain[t][:, cols], ALU.subtract
                 )
 
-        z_planes = [sb("z_planes%d" % h, [P, PACK, HALF], F32) for h in range(2)]
-        for h, cols in enumerate(HALVES):
-            for t in range(PACK):
-                if h == 0:
-                    for tt, part, acc in y_parts:
-                        if tt == t:
-                            nc.scalar.activation(y_gained[t][:, part], acc[:], ACT.Copy, scale=gain[:, t : t + 1])
-                nc.scalar.activation(squash[t][:, cols], diff[t][:, cols], ACT.Tanh, bias=no_bias[:])
-                nc.vector.tensor_tensor(
-                    z_planes[h][:, t, :], y_gained[t][:].indirect(entries(l2, cols)), squash[t][:, cols], ALU.mult
-                )
+        def gained(t):
+            for tt, cols, acc in y_parts:
+                if tt == t:
+                    nc.scalar.activation(y_gained[t][:, cols], acc[:], ACT.Copy, scale=gain[:, t : t + 1])
+
+        def gated(t, h):
+            cols = HALVES[h]
+            nc.scalar.activation(squash[t][:, cols], diff[t][:, cols], ACT.Tanh, bias=no_bias[:])
+            nc.vector.tensor_tensor(
+                z_planes[h][:, t, :], y_gained[t][:].indirect(entries(l2, cols)), squash[t][:, cols], ALU.mult
+            )
+
+        difference(0)
+        for t in range(PACK - 1):
+            difference(t + 1)
+            gained(t)
+            gated(t, 0)
+            if t == 0:
+                gated(0, 1)
+        gained(3)
+        gated(3, 0)
+        for t in range(1, PACK):
+            gated(t, 1)
 
         z_codes = sb("z_codes", [P, S], I32)
         z_bytes = sb("z_bytes", [P, S], U8)
@@ -190,8 +205,8 @@ def tile_picked_layfdifkinda_none_po_kernel(
                 acc = bank("h%d_%d" % (t, h), (5 + 4 * h + t) % 8, HALF)
                 product(acc, w2_codes, w2_bytes, t, z_codes, z_bytes, cols)
                 nc.scalar.copy(h_window[t][:, cols], acc[:])
-        fetch_factor(2, "squash2")
-        fetch_factor(3, "z_grouped1")
+        fetch_factor(2, "z_planes0")
+        fetch_factor(3, "z_planes1")
 
         out_rows = out_0.rearrange("(p t) j -> p t j", t=PACK)
         out_words = out_1[0].rearrange("p n t -> p (n t)").bitcast(I32)
@@ -210,11 +225,13 @@ def tile_picked_layfdifkinda_none_po_kernel(
                 nc.vector.tensor_tensor(
                     planes[:, t, :], tabs[t][:].indirect(entries(l4, cols)), scaled[t][:, cols], ALU.add
                 )
-            nc.sync.dma_start(out_rows[:, :, cols], planes[:])
             grouped = sb("o_grouped%d" % c, [P, width * PACK], BF16)
             if c + 1 < len(OUT_CHUNKS):
+                nc.sync.dma_start(out_rows[:, :, cols], planes[:])
                 interleave(nc.scalar.copy, grouped, planes)
             else:
+                nc.sync.dma_start(out_rows[:, 0:2, cols], planes[:, 0:2, :])
+                nc.sync.dma_start(out_rows[:, 2:4, cols], planes[:, 2:4, :])
                 pairs = grouped[:].rearrange("p (n u e) -> p u n e", u=2, e=2)
                 nc.scalar.copy(pairs[:, 0], planes[:, 0:2, :].rearrange("p e n -> p n e"))
                 nc.vector.tensor_copy(pairs[:, 1], planes[:, 2:4, :].rearrange("p e n -> p n e"))
@@ -222,4 +239,4 @@ def tile_picked_layfdifkinda_none_po_kernel(
             nc.sync.dma_start(out_words[:, cols], o_codes[:, cols])
         for q in range(4):
             queue = nc.sync if q % 2 else nc.scalar
-            queue.dma_start(out_2[0, 4 * q : 4 * q + 4, :].bitcast(I32), o_bytes[32 * q : 32 * q + 4, :].bitcast(I32))
+            queue.dma_start(out_2[0, q:16:4, :].bitcast(I32), o_bytes[q:P:32, :].bitcast(I32))

@@ -20,6 +20,7 @@ HALF = S // 2
 FLOPS = 2 * 2 * 512 * 512 * 512
 
 HALVES = [slice(0, 256), slice(256, 512)]
+WHOLE = [slice(0, 512)]
 OUT_CHUNKS = [slice(0, 256), slice(256, 384), slice(384, 512)]
 
 
@@ -57,9 +58,14 @@ def tile_picked_layfdifkinda_none_po_kernel(
 
         tab_rows = tab.rearrange("(p t) j -> p t j", t=PACK)
 
-        def load_tab(t, tag):
-            rows = sb("tab%d" % t, [P, S], F32, tag)
-            nc.sync.dma_start(rows[:], tab_rows[:, t, :])
+        def wide_window(name):
+            window = sb(name, [P, 2 * S], F32)
+            nc.vector.memset(window[:, S:].bitcast(I32), 0)
+            return window
+
+        def load_tab(t):
+            rows = wide_window("tab0") if t == 0 else sb("tab%d" % t, [P, S], F32)
+            nc.sync.dma_start(rows[:, :S], tab_rows[:, t, :])
             return rows
 
         def deal(name, raw, dtype, run, tag=None):
@@ -100,44 +106,45 @@ def tile_picked_layfdifkinda_none_po_kernel(
         nc.scalar.activation(no_bias[:], zero[:], ACT.Tanh)
 
         tabs = [None] * PACK
-        tabs[0] = load_tab(0, None)
+        tabs[0] = load_tab(0)
         l3 = load_list("l3", n3)
         l4 = load_list("l4", n4)
-        l0 = load_list("l0", offs)
-        load_scales(nc.sync, w_plane, w1_scales, range(3))
+        load_scales(nc.sync, w_plane, w1_scales)
         x_raw = load_words("x_raw", x_words, T, None)
-        load_scales(nc.sync, w_plane, w1_scales, range(3, 4))
-        load_scales(nc.sync, x_plane, x_scales)
+        l0 = load_list("l0", offs)
         w1_raw = load_words("w1_raw", w1_words, S, None)
-        tabs[1] = load_tab(1, None)
-        w2_raw = load_words("w2_raw", w2_words, S, None)
+        load_scales(nc.sync, x_plane, x_scales)
+        tabs[1] = load_tab(1)
         load_scales(nc.sync, w2_plane, w2_scales)
+        w2_raw = load_words("w2_raw", w2_words, S, None)
         l1 = load_list("l1", n1)
         l2 = load_list("l2", n2)
         gain = sb("gain", [P, PACK], F32)
         nc.gpsimd.dma_start(gain[:], gn.rearrange("(p t) o -> p (t o)", t=PACK))
         l5 = load_list("l5", n5)
+        tabs[2] = load_tab(2)
+        tabs[3] = load_tab(3)
 
         factors = {}
 
         def fetch_factor(t, tag=None):
             factors[t] = sb("factor%d" % t, [P, S], F32, tag)
-            for cols in HALVES:
+            for cols in HALVES if t else WHOLE:
                 nc.vector.tensor_copy(factors[t][:, cols], tabs[t][:].indirect(entries(l3, cols)))
 
         fetch_factor(0)
         term0 = sb("term0", [P, S], F32)
-        for cols in HALVES:
-            nc.vector.tensor_copy(term0[:, cols], tabs[0][:].indirect(entries(l4, cols)))
+        nc.vector.tensor_copy(term0[:], tabs[0][:].indirect(l4[:]))
         w1_bytes = deal("w1_bytes", w_plane, U8, 16)
         w1_codes = deal("w1_codes", w1_raw, I32, 4)
-        w2_codes = deal("w2_codes", w2_raw, I32, 4)
         w2_bytes = deal("w2_bytes", w2_plane, U8, 16)
+        w2_codes = deal("w2_codes", w2_raw, I32, 4)
 
         x_codes = sb("x_codes", [P, S], I32)
         x_bytes = sb("x_bytes", [P, S], U8)
-        y_window = [sb("y_window%d" % t, [P, S], F32) for t in range(PACK)]
-        y_plain = [sb("y_plain%d" % t, [P, S], F32) for t in range(PACK)]
+        y_window = [sb("y_window%d" % t, [P, 2 * S if t else S], F32) for t in range(PACK)]
+        y_last = sb("y_last", [P, S], F32)
+        y_plain = [y_window[t + 1][:, S:] for t in range(PACK - 1)] + [y_last[:]]
         y_gained = [sb("y_gained%d" % t, [P, S], F32) for t in range(PACK)]
         diff = [sb("diff%d" % t, [P, S], F32) for t in range(PACK)]
         squash = [sb("squash%d" % t, [P, S], F32) for t in range(PACK)]
@@ -154,8 +161,6 @@ def tile_picked_layfdifkinda_none_po_kernel(
             product(acc, w1_codes, w1_bytes, t, x_codes, x_bytes, slice(0, S))
             y_parts.append((t, slice(0, S), acc))
 
-        tabs[2] = load_tab(2, "x_raw")
-        tabs[3] = load_tab(3, "x_plane")
         fetch_factor(1)
 
         z_planes = [sb("z_planes%d" % h, [P, PACK, HALF], F32) for h in range(2)]
@@ -165,7 +170,7 @@ def tile_picked_layfdifkinda_none_po_kernel(
                 if tt == t:
                     nc.scalar.copy(y_window[t][:, cols], acc[:])
                     nc.scalar.copy(y_plain[t][:, cols], acc[:])
-            for cols in HALVES:
+            for cols in WHOLE if t else HALVES:
                 nc.vector.tensor_tensor(
                     diff[t][:, cols], y_window[t][:].indirect(entries(l1, cols)), y_plain[t][:, cols], ALU.subtract
                 )
@@ -182,21 +187,21 @@ def tile_picked_layfdifkinda_none_po_kernel(
                 z_planes[h][:, t, :], y_gained[t][:].indirect(entries(l2, cols)), squash[t][:, cols], ALU.mult
             )
 
-        difference(0)
         for t in range(PACK - 1):
-            difference(t + 1)
+            difference(t)
+        gained(0)
+        gated(0, 0)
+        gated(0, 1)
+        difference(3)
+        for t in range(1, PACK):
             gained(t)
             gated(t, 0)
-            if t == 0:
-                gated(0, 1)
-        gained(3)
-        gated(3, 0)
         for t in range(1, PACK):
             gated(t, 1)
 
         z_codes = sb("z_codes", [P, S], I32)
         z_bytes = sb("z_bytes", [P, S], U8)
-        h_window = [sb("h_window%d" % t, [P, S], F32) for t in range(PACK)]
+        h_window = y_window
         for h, cols in enumerate(HALVES):
             grouped = sb("z_grouped%d" % h, [P, HALF * PACK], BF16)
             interleave(nc.scalar.copy, grouped, z_planes[h])
@@ -214,12 +219,14 @@ def tile_picked_layfdifkinda_none_po_kernel(
         o_bytes = sb("o_bytes", [P, S], U8)
         scaled = [sb("scaled%d" % t, [P, S], F32) for t in range(PACK)]
         for c, cols in enumerate(OUT_CHUNKS):
+            if c < 2:
+                half = HALVES[c]
+                for t in range(PACK):
+                    nc.vector.tensor_tensor(
+                        scaled[t][:, half], h_window[t][:].indirect(entries(l5, half)), factors[t][:, half], ALU.mult
+                    )
             width = cols.stop - cols.start
             planes = sb("o_planes%d" % c, [P, PACK, width], F32)
-            for t in range(PACK):
-                nc.vector.tensor_tensor(
-                    scaled[t][:, cols], h_window[t][:].indirect(entries(l5, cols)), factors[t][:, cols], ALU.mult
-                )
             nc.vector.tensor_tensor(planes[:, 0, :], term0[:, cols], scaled[0][:, cols], ALU.add)
             for t in range(1, PACK):
                 nc.vector.tensor_tensor(

@@ -17,15 +17,20 @@ PACK = 4
 T = 2048
 S = 512
 HALF = S // 2
+GROUP = 16
+QUADRANT = 32
+BANKS = 8
+WORDS_A_LINE = 4
+BYTES_A_LINE = 16
 FLOPS = 2 * 2 * 512 * 512 * 512
 
-HALVES = [slice(0, 256), slice(256, 512)]
-WHOLE = [slice(0, 512)]
+WHOLE = [slice(0, S)]
+HALVES = [slice(0, HALF), slice(HALF, S)]
 OUT_CHUNKS = [slice(0, 256), slice(256, 384), slice(384, 512)]
 
 
-def entries(lst, cols):
-    return lst[:, cols.start // 16 : cols.stop // 16]
+def entries(list_tile, cols):
+    return list_tile[:, cols.start // GROUP : cols.stop // GROUP]
 
 
 def tile_picked_layfdifkinda_none_po_kernel(
@@ -43,148 +48,143 @@ def tile_picked_layfdifkinda_none_po_kernel(
             return psum.tile([P, width], F32, name=name, tag="bank%d" % number)
 
         def load_list(name, src):
-            lst = sb(name, [P, S // 16], U16)
-            nc.sync.dma_start(lst[:], src)
-            return lst
+            list_tile = sb(name, [P, S // GROUP], U16)
+            nc.sync.dma_start(list_tile[:], src)
+            return list_tile
 
-        def load_words(name, src, width, tag):
-            words = sb(name, [P, width], I32, tag)
+        def load_words(name, src, width):
+            words = sb(name, [P, width], I32)
             nc.sync.dma_start(words[:], src[0].rearrange("p n t -> p (n t)").bitcast(I32))
             return words
 
-        def load_scales(queue, plane, src, quadrants=range(4)):
-            for q in quadrants:
-                queue.dma_start(plane[q:P:32, :].bitcast(I32), src[0, q:16:4, :].bitcast(I32))
+        def load_scales(plane, src):
+            for r in range(PACK):
+                nc.sync.dma_start(plane[r:P:QUADRANT, :].bitcast(I32), src[0, r : PACK * PACK : PACK, :].bitcast(I32))
 
         tab_rows = tab.rearrange("(p t) j -> p t j", t=PACK)
 
-        def wide_window(name):
-            window = sb(name, [P, 2 * S], F32)
-            nc.vector.memset(window[:, S:].bitcast(I32), 0)
+        def load_tab(t, window):
+            nc.sync.dma_start(window[:, :S], tab_rows[:, t, :])
             return window
 
-        def load_tab(t):
-            rows = wide_window("tab0") if t == 0 else sb("tab%d" % t, [P, S], F32)
-            nc.sync.dma_start(rows[:, :S], tab_rows[:, t, :])
-            return rows
-
-        def deal(name, raw, dtype, run, tag=None):
-            dealt = sb(name, [P, S], dtype, tag)
-            nc.gpsimd.tensor_copy(
+        def deal(engine, name, raw, dtype, run):
+            dealt = sb(name, [P, S], dtype)
+            engine.tensor_copy(
                 dealt[:].rearrange("p (t c i) -> p c t i", t=PACK, i=run),
                 raw[:].rearrange("p (c i t) -> p c t i", t=PACK, i=run),
             )
             return dealt
 
-        def product(acc, w_words, w_scales, t, a_words, a_scales, cols):
-            rows = slice(P * t, P * (t + 1))
+        def product(acc, w_codes, w_bytes, t, a_codes, a_bytes, cols):
+            w_cols = slice(P * t, P * (t + 1))
             nc.tensor.matmul_mx(
                 out=acc[:],
-                lhsT=w_words[:, rows].bitcast(FP8X4),
-                lhsT_scale=w_scales[:, rows],
-                rhs=a_words[:, cols].bitcast(FP8X4),
-                rhs_scale=a_scales[:, cols],
+                lhsT=w_codes[:, w_cols].bitcast(FP8X4),
+                lhsT_scale=w_bytes[:, w_cols],
+                rhs=a_codes[:, cols].bitcast(FP8X4),
+                rhs_scale=a_bytes[:, cols],
                 start=True,
                 stop=True,
             )
 
-        def interleave(engine_copy, grouped, planes):
-            engine_copy(
-                grouped[:].rearrange("p (c i t) -> p c t i", i=4, t=PACK),
-                planes[:].rearrange("p t (c i) -> p c t i", i=4),
+        def interleave(grouped, slices):
+            nc.scalar.copy(
+                grouped[:].rearrange("p (c i t) -> p c t i", i=WORDS_A_LINE, t=PACK),
+                slices[:].rearrange("p t (c i) -> p c t i", i=WORDS_A_LINE),
             )
 
         x_plane = sb("x_plane", [P, T], U8)
-        w_plane = sb("w_plane", [P, S], U8)
+        w1_plane = sb("w1_plane", [P, S], U8)
         w2_plane = sb("w2_plane", [P, S], U8)
         zero = sb("zero", [P, 1], F32)
         no_bias = sb("no_bias", [P, 1], F32)
-        nc.gpsimd.memset(w_plane[:].bitcast(I32), 0)
+        nc.gpsimd.memset(w1_plane[:].bitcast(I32), 0)
         nc.gpsimd.memset(x_plane[:].bitcast(I32), 0)
         nc.gpsimd.memset(w2_plane[:].bitcast(I32), 0)
         nc.vector.memset(zero[:], 0.0)
         nc.scalar.activation(no_bias[:], zero[:], ACT.Tanh)
 
         tabs = [None] * PACK
-        tabs[0] = load_tab(0)
-        l3 = load_list("l3", n3)
-        l4 = load_list("l4", n4)
-        load_scales(nc.sync, w_plane, w1_scales)
-        x_raw = load_words("x_raw", x_words, T, None)
-        l0 = load_list("l0", offs)
-        w1_raw = load_words("w1_raw", w1_words, S, None)
-        load_scales(nc.sync, x_plane, x_scales)
-        tabs[1] = load_tab(1)
-        load_scales(nc.sync, w2_plane, w2_scales)
-        w2_raw = load_words("w2_raw", w2_words, S, None)
-        l1 = load_list("l1", n1)
-        l2 = load_list("l2", n2)
+        tab0_window = sb("tab0", [P, 2 * S], F32)
+        nc.vector.memset(tab0_window[:, S:].bitcast(I32), 0)
+        tabs[0] = load_tab(0, tab0_window)
+        list3 = load_list("list3", n3)
+        list4 = load_list("list4", n4)
+        load_scales(w1_plane, w1_scales)
+        x_raw = load_words("x_raw", x_words, T)
+        picks = load_list("picks", offs)
+        load_scales(x_plane, x_scales)
+        w1_raw = load_words("w1_raw", w1_words, S)
+        tabs[1] = load_tab(1, sb("tab1", [P, S], F32))
+        w2_raw = load_words("w2_raw", w2_words, S)
+        list1 = load_list("list1", n1)
+        load_scales(w2_plane, w2_scales)
+        list2 = load_list("list2", n2)
         gain = sb("gain", [P, PACK], F32)
         nc.gpsimd.dma_start(gain[:], gn.rearrange("(p t) o -> p (t o)", t=PACK))
-        l5 = load_list("l5", n5)
-        tabs[2] = load_tab(2)
-        tabs[3] = load_tab(3)
+        list5 = load_list("list5", n5)
+        tabs[2] = load_tab(2, sb("tab2", [P, S], F32))
+        tabs[3] = load_tab(3, sb("tab3", [P, S], F32))
 
-        factors = {}
+        factors = [None] * PACK
 
-        def fetch_factor(t, tag=None):
+        def fetch_factor(t, pieces, tag=None):
             factors[t] = sb("factor%d" % t, [P, S], F32, tag)
-            for cols in HALVES if t else WHOLE:
-                nc.vector.tensor_copy(factors[t][:, cols], tabs[t][:].indirect(entries(l3, cols)))
+            for cols in pieces:
+                nc.vector.tensor_copy(factors[t][:, cols], tabs[t][:].indirect(entries(list3, cols)))
 
-        fetch_factor(0)
+        fetch_factor(0, WHOLE)
         term0 = sb("term0", [P, S], F32)
-        nc.vector.tensor_copy(term0[:], tabs[0][:].indirect(l4[:]))
-        w1_bytes = deal("w1_bytes", w_plane, U8, 16)
-        w1_codes = deal("w1_codes", w1_raw, I32, 4)
-        w2_bytes = deal("w2_bytes", w2_plane, U8, 16)
-        w2_codes = deal("w2_codes", w2_raw, I32, 4)
+        nc.vector.tensor_copy(term0[:], tabs[0][:].indirect(list4[:]))
+        w1_bytes = deal(nc.gpsimd, "w1_bytes", w1_plane, U8, BYTES_A_LINE)
+        w1_codes = deal(nc.gpsimd, "w1_codes", w1_raw, I32, WORDS_A_LINE)
+        w2_codes = deal(nc.gpsimd, "w2_codes", w2_raw, I32, WORDS_A_LINE)
 
         x_codes = sb("x_codes", [P, S], I32)
         x_bytes = sb("x_bytes", [P, S], U8)
-        y_window = [sb("y_window%d" % t, [P, 2 * S if t else S], F32) for t in range(PACK)]
+        windows = [sb("window%d" % t, [P, 2 * S if t else S], F32) for t in range(PACK)]
         y_last = sb("y_last", [P, S], F32)
-        y_plain = [y_window[t + 1][:, S:] for t in range(PACK - 1)] + [y_last[:]]
+        y_plain = [windows[t + 1][:, S:] for t in range(PACK - 1)] + [y_last[:]]
         y_gained = [sb("y_gained%d" % t, [P, S], F32) for t in range(PACK)]
         diff = [sb("diff%d" % t, [P, S], F32) for t in range(PACK)]
         squash = [sb("squash%d" % t, [P, S], F32) for t in range(PACK)]
 
-        y_parts = []
-        nc.vector.tensor_copy(x_codes[:].bitcast(U32), x_raw[:].bitcast(U32).indirect(l0[:]))
+        y_banks = [[] for t in range(PACK)]
+        nc.vector.tensor_copy(x_codes[:].bitcast(U32), x_raw[:].bitcast(U32).indirect(picks[:]))
         for h, cols in enumerate(HALVES):
-            nc.vector.tensor_copy(x_bytes[:, cols], x_plane[:].indirect(entries(l0, cols)))
+            nc.vector.tensor_copy(x_bytes[:, cols], x_plane[:].indirect(entries(picks, cols)))
             acc = bank("y0_%d" % h, h, HALF)
             product(acc, w1_codes, w1_bytes, 0, x_codes, x_bytes, cols)
-            y_parts.append((0, cols, acc))
+            y_banks[0].append((cols, acc))
         for t in range(1, PACK):
             acc = bank("y%d" % t, t + 1, S)
-            product(acc, w1_codes, w1_bytes, t, x_codes, x_bytes, slice(0, S))
-            y_parts.append((t, slice(0, S), acc))
+            product(acc, w1_codes, w1_bytes, t, x_codes, x_bytes, WHOLE[0])
+            y_banks[t].append((WHOLE[0], acc))
+        y_bank_count = PACK + 1
 
-        fetch_factor(1)
+        fetch_factor(1, HALVES)
+        w2_bytes = deal(nc.vector, "w2_bytes", w2_plane, U8, BYTES_A_LINE)
 
-        z_planes = [sb("z_planes%d" % h, [P, PACK, HALF], F32) for h in range(2)]
+        z_slices = [sb("z_slices%d" % h, [P, PACK, HALF], F32) for h in range(len(HALVES))]
 
         def difference(t):
-            for tt, cols, acc in y_parts:
-                if tt == t:
-                    nc.scalar.copy(y_window[t][:, cols], acc[:])
-                    nc.scalar.copy(y_plain[t][:, cols], acc[:])
-            for cols in WHOLE if t else HALVES:
+            for cols, acc in y_banks[t]:
+                nc.scalar.copy(windows[t][:, cols], acc[:])
+                nc.scalar.copy(y_plain[t][:, cols], acc[:])
+            for cols, acc in y_banks[t]:
                 nc.vector.tensor_tensor(
-                    diff[t][:, cols], y_window[t][:].indirect(entries(l1, cols)), y_plain[t][:, cols], ALU.subtract
+                    diff[t][:, cols], windows[t][:].indirect(entries(list1, cols)), y_plain[t][:, cols], ALU.subtract
                 )
 
         def gained(t):
-            for tt, cols, acc in y_parts:
-                if tt == t:
-                    nc.scalar.activation(y_gained[t][:, cols], acc[:], ACT.Copy, scale=gain[:, t : t + 1])
+            for cols, acc in y_banks[t]:
+                nc.scalar.activation(y_gained[t][:, cols], acc[:], ACT.Copy, scale=gain[:, t : t + 1])
 
         def gated(t, h):
             cols = HALVES[h]
             nc.scalar.activation(squash[t][:, cols], diff[t][:, cols], ACT.Tanh, bias=no_bias[:])
             nc.vector.tensor_tensor(
-                z_planes[h][:, t, :], y_gained[t][:].indirect(entries(l2, cols)), squash[t][:, cols], ALU.mult
+                z_slices[h][:, t, :], y_gained[t][:].indirect(entries(list2, cols)), squash[t][:, cols], ALU.mult
             )
 
         for t in range(PACK - 1):
@@ -192,7 +192,7 @@ def tile_picked_layfdifkinda_none_po_kernel(
         gained(0)
         gated(0, 0)
         gated(0, 1)
-        difference(3)
+        difference(PACK - 1)
         for t in range(1, PACK):
             gained(t)
             gated(t, 0)
@@ -201,49 +201,48 @@ def tile_picked_layfdifkinda_none_po_kernel(
 
         z_codes = sb("z_codes", [P, S], I32)
         z_bytes = sb("z_bytes", [P, S], U8)
-        h_window = y_window
         for h, cols in enumerate(HALVES):
             grouped = sb("z_grouped%d" % h, [P, HALF * PACK], BF16)
-            interleave(nc.scalar.copy, grouped, z_planes[h])
+            interleave(grouped, z_slices[h])
             nc.vector.quantize_mx(out=z_codes[:, cols].bitcast(FP8X4), scales=z_bytes[:, cols], in_=grouped[:])
             for t in range(PACK):
-                acc = bank("h%d_%d" % (t, h), (5 + 4 * h + t) % 8, HALF)
+                acc = bank("h%d_%d" % (t, h), (y_bank_count + PACK * h + t) % BANKS, HALF)
                 product(acc, w2_codes, w2_bytes, t, z_codes, z_bytes, cols)
-                nc.scalar.copy(h_window[t][:, cols], acc[:])
-        fetch_factor(2, "z_planes0")
-        fetch_factor(3, "z_planes1")
+                nc.scalar.copy(windows[t][:, cols], acc[:])
+        fetch_factor(2, HALVES, "z_slices0")
+        fetch_factor(3, HALVES, "z_slices1")
 
         out_rows = out_0.rearrange("(p t) j -> p t j", t=PACK)
         out_words = out_1[0].rearrange("p n t -> p (n t)").bitcast(I32)
-        o_codes = sb("o_codes", [P, S], I32)
-        o_bytes = sb("o_bytes", [P, S], U8)
+        out_codes = sb("out_codes", [P, S], I32)
+        out_bytes = sb("out_bytes", [P, S], U8)
         scaled = [sb("scaled%d" % t, [P, S], F32) for t in range(PACK)]
         for c, cols in enumerate(OUT_CHUNKS):
-            if c < 2:
-                half = HALVES[c]
+            if cols.start % HALF == 0:
+                half = HALVES[cols.start // HALF]
                 for t in range(PACK):
                     nc.vector.tensor_tensor(
-                        scaled[t][:, half], h_window[t][:].indirect(entries(l5, half)), factors[t][:, half], ALU.mult
+                        scaled[t][:, half], windows[t][:].indirect(entries(list5, half)), factors[t][:, half], ALU.mult
                     )
             width = cols.stop - cols.start
-            planes = sb("o_planes%d" % c, [P, PACK, width], F32)
-            nc.vector.tensor_tensor(planes[:, 0, :], term0[:, cols], scaled[0][:, cols], ALU.add)
+            out_slices = sb("out_slices%d" % c, [P, PACK, width], F32)
+            nc.vector.tensor_tensor(out_slices[:, 0, :], term0[:, cols], scaled[0][:, cols], ALU.add)
             for t in range(1, PACK):
                 nc.vector.tensor_tensor(
-                    planes[:, t, :], tabs[t][:].indirect(entries(l4, cols)), scaled[t][:, cols], ALU.add
+                    out_slices[:, t, :], tabs[t][:].indirect(entries(list4, cols)), scaled[t][:, cols], ALU.add
                 )
-            grouped = sb("o_grouped%d" % c, [P, width * PACK], BF16)
-            if c + 1 < len(OUT_CHUNKS):
-                nc.sync.dma_start(out_rows[:, :, cols], planes[:])
-                interleave(nc.scalar.copy, grouped, planes)
+            grouped = sb("out_grouped%d" % c, [P, width * PACK], BF16)
+            if cols.stop < S:
+                nc.sync.dma_start(out_rows[:, :, cols], out_slices[:])
+                interleave(grouped, out_slices)
             else:
-                nc.sync.dma_start(out_rows[:, 0:2, cols], planes[:, 0:2, :])
-                nc.sync.dma_start(out_rows[:, 2:4, cols], planes[:, 2:4, :])
+                nc.sync.dma_start(out_rows[:, 0:2, cols], out_slices[:, 0:2, :])
+                nc.sync.dma_start(out_rows[:, 2:4, cols], out_slices[:, 2:4, :])
                 pairs = grouped[:].rearrange("p (n u e) -> p u n e", u=2, e=2)
-                nc.scalar.copy(pairs[:, 0], planes[:, 0:2, :].rearrange("p e n -> p n e"))
-                nc.vector.tensor_copy(pairs[:, 1], planes[:, 2:4, :].rearrange("p e n -> p n e"))
-            nc.vector.quantize_mx(out=o_codes[:, cols].bitcast(FP8X4), scales=o_bytes[:, cols], in_=grouped[:])
-            nc.sync.dma_start(out_words[:, cols], o_codes[:, cols])
-        for q in range(4):
-            queue = nc.sync if q % 2 else nc.scalar
-            queue.dma_start(out_2[0, q:16:4, :].bitcast(I32), o_bytes[q:P:32, :].bitcast(I32))
+                nc.scalar.copy(pairs[:, 0], out_slices[:, 0:2, :].rearrange("p e n -> p n e"))
+                nc.vector.tensor_copy(pairs[:, 1], out_slices[:, 2:4, :].rearrange("p e n -> p n e"))
+            nc.vector.quantize_mx(out=out_codes[:, cols].bitcast(FP8X4), scales=out_bytes[:, cols], in_=grouped[:])
+            nc.sync.dma_start(out_words[:, cols], out_codes[:, cols])
+        for r in range(PACK):
+            queue = nc.sync if r % 2 else nc.scalar
+            queue.dma_start(out_2[0, r : PACK * PACK : PACK, :].bitcast(I32), out_bytes[r:P:QUADRANT, :].bitcast(I32))

from contextlib import ExitStack

import concourse.mybir as mybir

F32 = mybir.dt.float32
BF16 = mybir.dt.bfloat16
I32 = mybir.dt.int32
U32 = mybir.dt.uint32
U16 = mybir.dt.uint16
U8 = mybir.dt.uint8
FP8X4 = mybir.dt.float8_e4m3fn_x4
ALU = mybir.AluOpType
ACT = mybir.ActivationFunctionType

P = 128
PACK = 4
T = 2048
S = 512
HALF = S // 2
GROUP = 16
QUADRANT = 32
BANKS = 8
WORDS_A_LINE = 4
BYTES_A_LINE = 16
FLOPS = 2 * 2 * 512 * 512 * 512

WHOLE = [slice(0, S)]
HALVES = [slice(0, HALF), slice(HALF, S)]
OUT_CHUNKS = [slice(0, 256), slice(256, 384), slice(384, 512)]


def entries(list_tile, cols):
    return list_tile[:, cols.start // GROUP : cols.stop // GROUP]


def tile_picked_layfdifkinda_none_po_kernel(
    tc, x_words, x_scales, w1_words, w1_scales, gn, w2_words, w2_scales, tab, offs, n1, n2, n3, n4, n5, out_0, out_1, out_2
):
    nc = tc.nc
    with ExitStack() as ctx:
        keep = ctx.enter_context(tc.tile_pool(name="keep", bufs=1))
        psum = ctx.enter_context(tc.psum_pool(name="psum", bufs=1))

        def sb(name, shape, dtype, tag=None):
            return keep.tile(shape, dtype, name=name, tag=tag or name, align_bytes=64)

        def bank(name, number, width):
            return psum.tile([P, width], F32, name=name, tag="bank%d" % number)

        def load_list(name, src):
            list_tile = sb(name, [P, S // GROUP], U16)
            nc.sync.dma_start(list_tile[:], src)
            return list_tile

        def load_words(name, src, width):
            words = sb(name, [P, width], I32)
            nc.sync.dma_start(words[:], src[0].rearrange("p n t -> p (n t)").bitcast(I32))
            return words

        def load_scales(plane, src):
            for r in range(PACK):
                nc.sync.dma_start(plane[r:P:QUADRANT, :].bitcast(I32), src[0, r : PACK * PACK : PACK, :].bitcast(I32))

        tab_rows = tab.rearrange("(p t) j -> p t j", t=PACK)

        def load_tab(t, window):
            nc.sync.dma_start(window[:, :S], tab_rows[:, t, :])
            return window

        def deal(engine, name, raw, dtype, run):
            dealt = sb(name, [P, S], dtype)
            engine.tensor_copy(
                dealt[:].rearrange("p (t c i) -> p c t i", t=PACK, i=run),
                raw[:].rearrange("p (c i t) -> p c t i", t=PACK, i=run),
            )
            return dealt

        def product(acc, w_codes, w_bytes, t, a_codes, a_bytes, cols):
            w_cols = slice(P * t, P * (t + 1))
            nc.tensor.matmul_mx(
                out=acc[:],
                lhsT=w_codes[:, w_cols].bitcast(FP8X4),
                lhsT_scale=w_bytes[:, w_cols],
                rhs=a_codes[:, cols].bitcast(FP8X4),
                rhs_scale=a_bytes[:, cols],
                start=True,
                stop=True,
            )

        def interleave(grouped, slices):
            nc.scalar.copy(
                grouped[:].rearrange("p (c i t) -> p c t i", i=WORDS_A_LINE, t=PACK),
                slices[:].rearrange("p t (c i) -> p c t i", i=WORDS_A_LINE),
            )

        x_plane = sb("x_plane", [P, T], U8)
        w1_plane = sb("w1_plane", [P, S], U8)
        w2_plane = sb("w2_plane", [P, S], U8)
        zero = sb("zero", [P, 1], F32)
        no_bias = sb("no_bias", [P, 1], F32)
        nc.gpsimd.memset(w1_plane[:].bitcast(I32), 0)
        nc.gpsimd.memset(x_plane[:].bitcast(I32), 0)
        nc.gpsimd.memset(w2_plane[:].bitcast(I32), 0)
        nc.vector.memset(zero[:], 0.0)
        nc.scalar.activation(no_bias[:], zero[:], ACT.Tanh)

        tabs = [None] * PACK
        tab0_window = sb("tab0", [P, 2 * S], F32)
        nc.vector.memset(tab0_window[:, S:].bitcast(I32), 0)
        tabs[0] = load_tab(0, tab0_window)
        list3 = load_list("list3", n3)
        list4 = load_list("list4", n4)
        load_scales(w1_plane, w1_scales)
        x_raw = load_words("x_raw", x_words, T)
        picks = load_list("picks", offs)
        load_scales(x_plane, x_scales)
        w1_raw = load_words("w1_raw", w1_words, S)
        tabs[1] = load_tab(1, sb("tab1", [P, S], F32))
        w2_raw = load_words("w2_raw", w2_words, S)
        list1 = load_list("list1", n1)
        load_scales(w2_plane, w2_scales)
        list2 = load_list("list2", n2)
        gain = sb("gain", [P, PACK], F32)
        nc.gpsimd.dma_start(gain[:], gn.rearrange("(p t) o -> p (t o)", t=PACK))
        list5 = load_list("list5", n5)
        tabs[2] = load_tab(2, sb("tab2", [P, S], F32))
        tabs[3] = load_tab(3, sb("tab3", [P, S], F32))

        factors = [None] * PACK

        def fetch_factor(t, pieces, tag=None):
            factors[t] = sb("factor%d" % t, [P, S], F32, tag)
            for cols in pieces:
                nc.vector.tensor_copy(factors[t][:, cols], tabs[t][:].indirect(entries(list3, cols)))

        fetch_factor(0, WHOLE)
        term0 = sb("term0", [P, S], F32)
        nc.vector.tensor_copy(term0[:], tabs[0][:].indirect(list4[:]))
        w1_bytes = deal(nc.gpsimd, "w1_bytes", w1_plane, U8, BYTES_A_LINE)
        w1_codes = deal(nc.gpsimd, "w1_codes", w1_raw, I32, WORDS_A_LINE)
        w2_codes = deal(nc.gpsimd, "w2_codes", w2_raw, I32, WORDS_A_LINE)

        x_codes = sb("x_codes", [P, S], I32)
        x_bytes = sb("x_bytes", [P, S], U8)
        windows = [sb("window%d" % t, [P, 2 * S if t else S], F32) for t in range(PACK)]
        y_last = sb("y_last", [P, S], F32)
        y_plain = [windows[t + 1][:, S:] for t in range(PACK - 1)] + [y_last[:]]
        y_gained = [sb("y_gained%d" % t, [P, S], F32) for t in range(PACK)]
        diff = [sb("diff%d" % t, [P, S], F32) for t in range(PACK)]
        squash = [sb("squash%d" % t, [P, S], F32) for t in range(PACK)]

        y_banks = [[] for t in range(PACK)]
        nc.vector.tensor_copy(x_codes[:].bitcast(U32), x_raw[:].bitcast(U32).indirect(picks[:]))
        for h, cols in enumerate(HALVES):
            nc.vector.tensor_copy(x_bytes[:, cols], x_plane[:].indirect(entries(picks, cols)))
            acc = bank("y0_%d" % h, h, HALF)
            product(acc, w1_codes, w1_bytes, 0, x_codes, x_bytes, cols)
            y_banks[0].append((cols, acc))
        for t in range(1, PACK):
            acc = bank("y%d" % t, t + 1, S)
            product(acc, w1_codes, w1_bytes, t, x_codes, x_bytes, WHOLE[0])
            y_banks[t].append((WHOLE[0], acc))
        y_bank_count = PACK + 1

        fetch_factor(1, HALVES)
        w2_bytes = deal(nc.vector, "w2_bytes", w2_plane, U8, BYTES_A_LINE)

        z_slices = [sb("z_slices%d" % h, [P, PACK, HALF], F32) for h in range(len(HALVES))]

        def difference(t):
            for cols, acc in y_banks[t]:
                nc.scalar.copy(windows[t][:, cols], acc[:])
                nc.scalar.copy(y_plain[t][:, cols], acc[:])
            for cols, acc in y_banks[t]:
                nc.vector.tensor_tensor(
                    diff[t][:, cols], windows[t][:].indirect(entries(list1, cols)), y_plain[t][:, cols], ALU.subtract
                )

        def gained(t):
            for cols, acc in y_banks[t]:
                nc.scalar.activation(y_gained[t][:, cols], acc[:], ACT.Copy, scale=gain[:, t : t + 1])

        def gated(t, h):
            cols = HALVES[h]
            nc.scalar.activation(squash[t][:, cols], diff[t][:, cols], ACT.Tanh, bias=no_bias[:])
            nc.vector.tensor_tensor(
                z_slices[h][:, t, :], y_gained[t][:].indirect(entries(list2, cols)), squash[t][:, cols], ALU.mult
            )

        for t in range(PACK - 1):
            difference(t)
        gained(0)
        gated(0, 0)
        gated(0, 1)
        difference(PACK - 1)
        for t in range(1, PACK):
            gained(t)
            gated(t, 0)
        for t in range(1, PACK):
            gated(t, 1)

        z_codes = sb("z_codes", [P, S], I32)
        z_bytes = sb("z_bytes", [P, S], U8)
        for h, cols in enumerate(HALVES):
            grouped = sb("z_grouped%d" % h, [P, HALF * PACK], BF16)
            interleave(grouped, z_slices[h])
            nc.vector.quantize_mx(out=z_codes[:, cols].bitcast(FP8X4), scales=z_bytes[:, cols], in_=grouped[:])
            for t in range(PACK):
                acc = bank("h%d_%d" % (t, h), (y_bank_count + PACK * h + t) % BANKS, HALF)
                product(acc, w2_codes, w2_bytes, t, z_codes, z_bytes, cols)
                nc.scalar.copy(windows[t][:, cols], acc[:])
        fetch_factor(2, HALVES, "z_slices0")
        fetch_factor(3, HALVES, "z_slices1")

        out_rows = out_0.rearrange("(p t) j -> p t j", t=PACK)
        out_words = out_1[0].rearrange("p n t -> p (n t)").bitcast(I32)
        out_codes = sb("out_codes", [P, S], I32)
        out_bytes = sb("out_bytes", [P, S], U8)
        scaled = [sb("scaled%d" % t, [P, S], F32) for t in range(PACK)]
        for c, cols in enumerate(OUT_CHUNKS):
            if cols.start % HALF == 0:
                half = HALVES[cols.start // HALF]
                for t in range(PACK):
                    nc.vector.tensor_tensor(
                        scaled[t][:, half], windows[t][:].indirect(entries(list5, half)), factors[t][:, half], ALU.mult
                    )
            width = cols.stop - cols.start
            out_slices = sb("out_slices%d" % c, [P, PACK, width], F32)
            nc.vector.tensor_tensor(out_slices[:, 0, :], term0[:, cols], scaled[0][:, cols], ALU.add)
            for t in range(1, PACK):
                nc.vector.tensor_tensor(
                    out_slices[:, t, :], tabs[t][:].indirect(entries(list4, cols)), scaled[t][:, cols], ALU.add
                )
            grouped = sb("out_grouped%d" % c, [P, width * PACK], BF16)
            if cols.stop < S:
                nc.sync.dma_start(out_rows[:, :, cols], out_slices[:])
                interleave(grouped, out_slices)
            else:
                nc.sync.dma_start(out_rows[:, 0:2, cols], out_slices[:, 0:2, :])
                nc.sync.dma_start(out_rows[:, 2:4, cols], out_slices[:, 2:4, :])
                pairs = grouped[:].rearrange("p (n u e) -> p u n e", u=2, e=2)
                nc.scalar.copy(pairs[:, 0], out_slices[:, 0:2, :].rearrange("p e n -> p n e"))
                nc.vector.tensor_copy(pairs[:, 1], out_slices[:, 2:4, :].rearrange("p e n -> p n e"))
            nc.vector.quantize_mx(out=out_codes[:, cols].bitcast(FP8X4), scales=out_bytes[:, cols], in_=grouped[:])
            nc.sync.dma_start(out_words[:, cols], out_codes[:, cols])
        for r in range(PACK):
            queue = nc.sync if r % 2 else nc.scalar
            queue.dma_start(out_2[0, r : PACK * PACK : PACK, :].bitcast(I32), out_bytes[r:P:QUADRANT, :].bitcast(I32))
